import numpy as np
import ml_dtypes


def mxq(x, axis, fmt="e4m3"):
    dtype, down = {"e4m3": (ml_dtypes.float8_e4m3fn, 7), "e5m2": (ml_dtypes.float8_e5m2, 14)}[fmt]
    v = np.moveaxis(np.asarray(x, np.float32).astype(ml_dtypes.bfloat16).astype(np.float64), axis, -1)
    blocks = v.reshape(v.shape[:-1] + (-1, 32))
    amax = np.abs(blocks).max(-1, keepdims=True)
    byte = np.maximum(np.where(amax > 0, np.frexp(amax)[1] - 1 + 127, 0) - down, 1)
    scale = np.exp2(byte - 127.0)
    codes = (blocks / scale).astype(np.float32).astype(dtype).astype(np.float64)
    return np.moveaxis((codes * scale).reshape(v.shape), -1, axis)


WIDE = False


def mx_kscale(k):
    if not WIDE:
        return np.ones(k)
    levels = np.array([10, -10, 5, -5, 0])
    if k % 512:
        return np.exp2(np.random.permutation(np.resize(levels, k // 32))).repeat(32)
    a = np.empty((k // 512, 16))
    for p in range(k // 512):
        a[p, :8] = np.random.permutation(np.resize(levels, 8))
        for g in range(8):
            far = levels[np.abs(levels - a[p, g]) >= 10]
            a[p, g + 8] = far[np.random.randint(len(far))]
    return np.exp2(a.ravel()).repeat(32)


def f64(x):
    return np.asarray(x).astype(np.float64)


def striped(idx):
    return np.tile(np.asarray(idx).reshape(-1, 16).T, (8, 1)).astype(np.uint16)


def unstriped(offs):
    return offs[:16].T.reshape(-1).astype(np.int64)


def striped8(idx):
    return np.asarray(idx).reshape(8, -1, 16).transpose(0, 2, 1).reshape(128, -1).astype(np.uint16)


def unstriped8(offs):
    return offs.reshape(8, 16, -1).transpose(0, 2, 1).reshape(8, -1).astype(np.int64)


def pick8(x, idx, run):
    r = np.arange(len(x))
    return x[r[:, None], idx[r % (8 * run) // run]]


E2M1 = np.array([0.0, 0.5, 1.0, 1.5, 2.0, 3.0, 4.0, 6.0, -0.0, -0.5, -1.0, -1.5, -2.0, -3.0, -4.0, -6.0])


def pack_weight(w, fmt):
    k, n = w.shape
    w = f64(np.asarray(w, np.float32).astype(ml_dtypes.bfloat16)).reshape(k // 32, 32, n)
    amax = np.abs(w).max(1)
    if fmt == "e4m3":
        byte = np.frexp(amax)[1] - 1 + 127 - 7
    else:
        mant, ex = np.frexp(amax / 6.0)
        byte = np.where(mant > 0.5, ex, ex - 1) + 127
    byte = np.clip(np.where(amax > 0, byte, 1), 1, 254)
    scaled = (w * np.exp2(127.0 - byte)[:, None, :]).reshape(k, n).astype(np.float32)
    by_word = np.ascontiguousarray(scaled.reshape(k // 512, 128, 4, n).transpose(0, 1, 3, 2))
    if fmt == "e4m3":
        words = by_word.astype(ml_dtypes.float8_e4m3fn).view(np.uint8)
    else:
        c = by_word.astype(ml_dtypes.float4_e2m1fn).view(np.uint8) & 0xF
        words = (c[..., 0::2] | (c[..., 1::2] << 4)).reshape(k // 512, 128, 2 * n)
    return np.ascontiguousarray(words), np.ascontiguousarray(byte.astype(np.uint8).reshape(k // 512, 16, n))


def unpack_weight(words, scales, fmt):
    g, _, n = scales.shape
    words = np.ascontiguousarray(words).reshape(g, 128, n, -1)
    if fmt == "e4m3":
        vals = words.view(ml_dtypes.float8_e4m3fn).astype(np.float64)
    else:
        nib = np.empty((g, 128, n, 4), np.uint8)
        nib[..., 0::2] = words & 0xF
        nib[..., 1::2] = words >> 4
        vals = E2M1[nib]
    vals = vals * np.repeat(np.exp2(scales.astype(np.float64) - 127.0), 8, axis=1)[..., None]
    return vals.transpose(0, 1, 3, 2).reshape(g * 512, n)


K, R, F, T, J, M = 512, 128, 512, 2048, 512, 256


def setup_inputs():
    n = np.random.standard_normal
    idx = np.random.permutation(T)[:J]
    idx2 = np.stack([np.random.permutation(J)[:M] for _ in range(8)])
    idx3 = np.stack([np.random.permutation(J)[:M] for _ in range(8)])
    fk = mx_kscale(K)
    tabp = pack_weight(n((K, T)) / fk[:, None], "e4m3")
    dtabp = pack_weight(n((K, T)) / fk[:, None], "e4m3")
    return {
        "tab_words": tabp[0],
        "tab_scales": tabp[1],
        "dtab_words": dtabp[0],
        "dtab_scales": dtabp[1],
        "w1": (n((K, R)) * 1 / np.sqrt(K) * fk[:, None]).astype(np.float32),
        "sharp": (np.random.uniform(0.1, 0.5, (1, M))).astype(np.float32),
        "og": (np.random.uniform(0.5, 2.0, (R, 1))).astype(np.float32),
        "base": (0.3 * n((R, M))).astype(np.float32),
        "offs": striped(idx),
        "offs2": striped8(idx2),
        "offs3": striped8(idx3),
    }


def reference(tab_words, tab_scales, dtab_words, dtab_scales, w1, sharp, og, base, offs, offs2, offs3):
    idx = unstriped(offs)
    idx2 = unstriped8(offs2)
    idx3 = unstriped8(offs3)
    tabu = unpack_weight(tab_words, tab_scales, "e4m3")
    dtabu = unpack_weight(dtab_words, dtab_scales, "e4m3")
    w1q = mxq(f64(w1), 0, "e4m3")
    tabidxg = tabu[:, idx]
    a = w1q.T @ tabidxg
    dtabidxg = dtabu[:, idx]
    ta = w1q.T @ dtabidxg
    dl = pick8(a, idx2, 16) - pick8(a, idx3, 16)
    u1 = np.exp(np.square(dl) * f64(sharp) * (-1.0))
    tdl = pick8(ta, idx2, 16) - pick8(ta, idx3, 16)
    tu1 = tdl * dl * 2.0 * f64(sharp) * (-1.0) * u1
    y = tu1 * f64(og) + f64(base)
    return y

@@ -1,0 +1,123 @@
+from contextlib import ExitStack
+
+import concourse.mybir as mybir
+
+K, R, T, J, M = 512, 128, 2048, 512, 256
+FLOPS = 2 * 2 * K * R * J
+
+F32 = mybir.dt.float32
+BF16 = mybir.dt.bfloat16
+I32 = mybir.dt.int32
+U32 = mybir.dt.uint32
+U16 = mybir.dt.uint16
+U8 = mybir.dt.uint8
+FP8X4 = mybir.dt.float8_e4m3fn_x4
+ALU = mybir.AluOpType
+ACT = mybir.ActivationFunctionType
+P = 128
+PACK = 4
+
+
+def tile_attend_tcpairnear_kernel(tc, tab_words, tab_scales, dtab_words, dtab_scales, w1, sharp, og, base, offs, offs2, offs3, out):
+    nc = tc.nc
+    with ExitStack() as ctx:
+        lists = ctx.enter_context(tc.tile_pool(name="lists", bufs=1))
+        keep = ctx.enter_context(tc.tile_pool(name="keep", bufs=1))
+        reuse = ctx.enter_context(tc.tile_pool(name="reuse", bufs=1))
+        psum = ctx.enter_context(tc.psum_pool(name="psum", bufs=1))
+
+        slot_list = lists.tile([P, J // 16], U16, name="slot_list")
+        left_list = lists.tile([P, M // 16], U16, name="left_list")
+        right_list = lists.tile([P, M // 16], U16, name="right_list")
+        nc.sync.dma_start(slot_list[:], offs)
+        tab_sb = keep.tile([P, T], I32, name="tab_sb")
+        nc.scalar.dma_start(tab_sb[:], tab_words[0].rearrange("p n t -> p (n t)").bitcast(I32))
+        nc.sync.dma_start(left_list[:], offs2)
+        nc.sync.dma_start(right_list[:], offs3)
+        w_raw = keep.tile([P, PACK, R], F32, name="w_raw")
+        nc.gpsimd.dma_start(w_raw[:], w1.rearrange("(p j) r -> p j r", j=PACK))
+
+        tab_plane = keep.tile([P, T], U8, name="tab_plane", tag="tab_plane_then_base")
+        dtab_plane = keep.tile([P, T], U8, name="dtab_plane")
+        nc.vector.memset(tab_plane[:].bitcast(I32), 0)
+        nc.vector.memset(dtab_plane[:].bitcast(I32), 0)
+
+        def load_plane(plane, scales, first_row):
+            rows = scales[0].bitcast(I32).rearrange("(q f) c -> f q c", f=4)
+            for f in range(4):
+                nc.sync.dma_start(plane[:].bitcast(I32)[first_row + f : P : 32, :], rows[f])
+
+        load_plane(tab_plane, tab_scales, 0)
+        load_plane(dtab_plane, dtab_scales, 4)
+
+        zeros = reuse.tile([P, P], F32, name="zeros", offset=0)
+        ident = keep.tile([P, P], F32, name="ident")
+        nc.gpsimd.memset(zeros[:], 0.0)
+        nc.gpsimd.affine_select(out=ident[:], in_=zeros[:], compare_op=ALU.not_equal, fill=1.0, base=0, pattern=[[-1, P]], channel_multiplier=1)
+        dtab_sb = reuse.tile([P, T], I32, name="dtab_sb", offset=0)
+        nc.sync.dma_start(dtab_sb[:], dtab_words[0].rearrange("p n t -> p (n t)").bitcast(I32))
+        sharp_col = keep.tile([P, 2], F32, name="sharp_col")
+        nc.gpsimd.dma_start(sharp_col[:], sharp.rearrange("o (p c) -> (o p) c", c=2))
+        og_col = keep.tile([P, 1], F32, name="og_col")
+        nc.gpsimd.dma_start(og_col[:], og)
+
+        tab_s = keep.tile([P, J], U8, name="tab_s", align_bytes=64)
+        nc.vector.tensor_copy(tab_s[:], tab_plane[:].indirect(slot_list[:]))
+        base_sb = keep.tile([P, M], F32, name="base_sb", tag="tab_plane_then_base")
+        nc.sync.dma_start(base_sb[:], base)
+        tab_w = keep.tile([P, J], U32, name="tab_w", align_bytes=64)
+        nc.vector.tensor_copy(tab_w[:], tab_sb[:].bitcast(U32).indirect(slot_list[:]))
+
+        w_bf = keep.tile([P, R, PACK], BF16, name="w_bf", tag="w_bf_then_scales", align_bytes=64)
+        nc.scalar.copy(w_bf[:], w_raw[:].rearrange("p j r -> p r j"))
+        w_codes = keep.tile([P, R], U32, name="w_codes", align_bytes=64)
+        w_scales = keep.tile([P, R], U8, name="w_scales", align_bytes=64)
+        nc.vector.quantize_mx(w_codes[:].bitcast(FP8X4), w_scales[:], w_bf[:].rearrange("p r j -> p (r j)"))
+        dtab_s = keep.tile([P, J], U8, name="dtab_s", tag="w_bf_then_scales", align_bytes=64)
+        nc.vector.tensor_copy(dtab_s[:], dtab_plane[:].indirect(slot_list[:]))
+
+        a_ps = psum.tile([P, J], F32, name="a_ps")
+        nc.tensor.matmul_mx(a_ps[:], lhsT=w_codes[:].bitcast(FP8X4), lhsT_scale=w_scales[:], rhs=tab_w[:].bitcast(FP8X4), rhs_scale=tab_s[:], start=True, stop=True)
+        a_sb = keep.tile([P, J], F32, name="a_sb")
+        nc.scalar.copy(a_sb[:], a_ps[:])
+
+        sharp_ps = psum.tile([P, 2, P], F32, name="sharp_ps")
+        for half in range(2):
+            nc.tensor.transpose(sharp_ps[:, half, :], sharp_col[:, half : half + 1].to_broadcast([P, P]), ident[:])
+        sharp_row = sharp_ps[:].rearrange("p c n -> p n c")
+
+        a_right = keep.tile([P, M], F32, name="a_right", tag="a_right_then_words", align_bytes=64)
+        dl = keep.tile([P, M], F32, name="dl")
+        nc.vector.tensor_copy(a_right[:], a_sb[:].indirect(right_list[:]))
+        nc.vector.tensor_tensor(dl[:], a_sb[:].indirect(left_list[:]), a_right[:], ALU.subtract)
+        sq = keep.tile([P, M], F32, name="sq")
+        nc.scalar.activation(sq[:], dl[:], ACT.Square)
+
+        dtab_w = keep.tile([P, J], U32, name="dtab_w", tag="a_right_then_words", align_bytes=64)
+        nc.vector.tensor_copy(dtab_w[:], dtab_sb[:].bitcast(U32).indirect(slot_list[:]))
+        ta_ps = psum.tile([P, J], F32, name="ta_ps")
+        nc.tensor.matmul_mx(ta_ps[:], lhsT=w_codes[:].bitcast(FP8X4), lhsT_scale=w_scales[:], rhs=dtab_w[:].bitcast(FP8X4), rhs_scale=dtab_s[4:P, :], start=True, stop=True)
+        ta_sb = keep.tile([P, J], F32, name="ta_sb")
+        nc.scalar.copy(ta_sb[:], ta_ps[:])
+
+        def pairs(t):
+            return t[:].rearrange("p (n c) -> p n c", c=2)
+
+        e = reuse.tile([P, M], F32, name="e", offset=0)
+        nc.vector.tensor_tensor(pairs(e), pairs(sq), sharp_row, ALU.mult)
+        u = keep.tile([P, M], F32, name="u")
+        nc.scalar.activation(u[:], e[:], ACT.Exp, scale=-1.0)
+        q = reuse.tile([P, M], F32, name="q", offset=4 * M)
+        nc.vector.scalar_tensor_tensor(pairs(q), pairs(dl), -2.0, sharp_row, ALU.mult, ALU.mult)
+        c = keep.tile([P, M], F32, name="c")
+        nc.vector.tensor_tensor(c[:], q[:], u[:], ALU.mult)
+
+        ta_right = keep.tile([P, M], F32, name="ta_right")
+        nc.vector.tensor_copy(ta_right[:], ta_sb[:].indirect(right_list[:]))
+        tdl = keep.tile([P, M], F32, name="tdl")
+        nc.vector.tensor_tensor(tdl[:], ta_sb[:].indirect(left_list[:]), ta_right[:], ALU.subtract)
+        m = keep.tile([P, M], F32, name="m")
+        nc.vector.tensor_tensor(m[:], c[:], tdl[:], ALU.mult)
+        y = keep.tile([P, M], F32, name="y")
+        nc.vector.scalar_tensor_tensor(y[:], m[:], og_col[:], base_sb[:], ALU.mult, ALU.add)
+        nc.sync.dma_start(out, y[:])

@@ -1,6 +1,7 @@
 from contextlib import ExitStack
 
 import concourse.mybir as mybir
+from concourse.masks import make_identity
 
 K, R, T, J, M = 512, 128, 2048, 512, 256
 FLOPS = 2 * 2 * K * R * J
@@ -30,15 +31,16 @@ def tile_attend_tcpairnear_kernel(tc, tab_words, tab_scales, dtab_words, dtab_sc
         left_list = lists.tile([P, M // 16], U16, name="left_list")
         right_list = lists.tile([P, M // 16], U16, name="right_list")
         nc.sync.dma_start(slot_list[:], offs)
+        w_raw = reuse.tile([P, PACK, R], F32, name="w_raw", offset=T)
+        nc.scalar.dma_start(w_raw[:], w1.rearrange("(p j) r -> p j r", j=PACK))
+        nc.sync.dma_start(left_list[:], offs2)
         tab_sb = keep.tile([P, T], I32, name="tab_sb")
         nc.scalar.dma_start(tab_sb[:], tab_words[0].rearrange("p n t -> p (n t)").bitcast(I32))
-        nc.sync.dma_start(left_list[:], offs2)
         nc.sync.dma_start(right_list[:], offs3)
-        w_raw = keep.tile([P, PACK, R], F32, name="w_raw")
-        nc.gpsimd.dma_start(w_raw[:], w1.rearrange("(p j) r -> p j r", j=PACK))
 
-        tab_plane = keep.tile([P, T], U8, name="tab_plane", tag="tab_plane_then_base")
-        dtab_plane = keep.tile([P, T], U8, name="dtab_plane")
+        late_at = 5 * T
+        tab_plane = reuse.tile([P, T], U8, name="tab_plane", offset=late_at)
+        dtab_plane = reuse.tile([P, T], U8, name="dtab_plane", offset=0)
         nc.vector.memset(tab_plane[:].bitcast(I32), 0)
         nc.vector.memset(dtab_plane[:].bitcast(I32), 0)
 
@@ -50,72 +52,70 @@ def tile_attend_tcpairnear_kernel(tc, tab_words, tab_scales, dtab_words, dtab_sc
         load_plane(tab_plane, tab_scales, 0)
         load_plane(dtab_plane, dtab_scales, 4)
 
-        zeros = reuse.tile([P, P], F32, name="zeros", offset=0)
         ident = keep.tile([P, P], F32, name="ident")
-        nc.gpsimd.memset(zeros[:], 0.0)
-        nc.gpsimd.affine_select(out=ident[:], in_=zeros[:], compare_op=ALU.not_equal, fill=1.0, base=0, pattern=[[-1, P]], channel_multiplier=1)
-        dtab_sb = reuse.tile([P, T], I32, name="dtab_sb", offset=0)
-        nc.sync.dma_start(dtab_sb[:], dtab_words[0].rearrange("p n t -> p (n t)").bitcast(I32))
-        sharp_col = keep.tile([P, 2], F32, name="sharp_col")
-        nc.gpsimd.dma_start(sharp_col[:], sharp.rearrange("o (p c) -> (o p) c", c=2))
-        og_col = keep.tile([P, 1], F32, name="og_col")
-        nc.gpsimd.dma_start(og_col[:], og)
+        make_identity(nc, ident[:])
 
-        tab_s = keep.tile([P, J], U8, name="tab_s", align_bytes=64)
-        nc.vector.tensor_copy(tab_s[:], tab_plane[:].indirect(slot_list[:]))
-        base_sb = keep.tile([P, M], F32, name="base_sb", tag="tab_plane_then_base")
-        nc.sync.dma_start(base_sb[:], base)
-        tab_w = keep.tile([P, J], U32, name="tab_w", align_bytes=64)
-        nc.vector.tensor_copy(tab_w[:], tab_sb[:].bitcast(U32).indirect(slot_list[:]))
-
-        w_bf = keep.tile([P, R, PACK], BF16, name="w_bf", tag="w_bf_then_scales", align_bytes=64)
+        w_bf = keep.tile([P, R, PACK], BF16, name="w_bf", align_bytes=64)
         nc.scalar.copy(w_bf[:], w_raw[:].rearrange("p j r -> p r j"))
+        dtab_sb = reuse.tile([P, T], I32, name="dtab_sb", offset=T)
+        nc.scalar.dma_start(dtab_sb[:], dtab_words[0].rearrange("p n t -> p (n t)").bitcast(I32))
         w_codes = keep.tile([P, R], U32, name="w_codes", align_bytes=64)
         w_scales = keep.tile([P, R], U8, name="w_scales", align_bytes=64)
         nc.vector.quantize_mx(w_codes[:].bitcast(FP8X4), w_scales[:], w_bf[:].rearrange("p r j -> p (r j)"))
-        dtab_s = keep.tile([P, J], U8, name="dtab_s", tag="w_bf_then_scales", align_bytes=64)
-        nc.vector.tensor_copy(dtab_s[:], dtab_plane[:].indirect(slot_list[:]))
 
-        a_ps = psum.tile([P, J], F32, name="a_ps")
+        tab_s = keep.tile([P, J], U8, name="tab_s", align_bytes=64)
+        nc.vector.tensor_copy(tab_s[:], tab_plane[:].indirect(slot_list[:]))
+        sharp_col = reuse.tile([P, 2], F32, name="sharp_col", offset=late_at)
+        nc.sync.dma_start(sharp_col[:], sharp.rearrange("o (p c) -> (o p) c", c=2))
+        og_col = reuse.tile([P, 1], F32, name="og_col", offset=late_at + 32)
+        nc.sync.dma_start(og_col[:], og)
+        base_sb = reuse.tile([P, M], F32, name="base_sb", offset=late_at + 64)
+        nc.sync.dma_start(base_sb[:], base)
+
+        tab_w = keep.tile([P, J], U32, name="tab_w", align_bytes=64)
+        nc.vector.tensor_copy(tab_w[:], tab_sb[:].bitcast(U32).indirect(slot_list[:]))
+        dtab_s = keep.tile([P, J], U8, name="dtab_s", align_bytes=64)
+        nc.vector.tensor_copy(dtab_s[:], dtab_plane[:].indirect(slot_list[:]))
+        dtab_w = keep.tile([P, J], U32, name="dtab_w", align_bytes=64)
+        nc.vector.tensor_copy(dtab_w[:], dtab_sb[:].bitcast(U32).indirect(slot_list[:]))
+
+        a_ps = psum.tile([P, J], F32, name="a_ps", tag="a_then_sharp")
         nc.tensor.matmul_mx(a_ps[:], lhsT=w_codes[:].bitcast(FP8X4), lhsT_scale=w_scales[:], rhs=tab_w[:].bitcast(FP8X4), rhs_scale=tab_s[:], start=True, stop=True)
         a_sb = keep.tile([P, J], F32, name="a_sb")
         nc.scalar.copy(a_sb[:], a_ps[:])
 
-        sharp_ps = psum.tile([P, 2, P], F32, name="sharp_ps")
+        sharp_ps = psum.tile([P, 2, P], F32, name="sharp_ps", tag="a_then_sharp")
         for half in range(2):
             nc.tensor.transpose(sharp_ps[:, half, :], sharp_col[:, half : half + 1].to_broadcast([P, P]), ident[:])
         sharp_row = sharp_ps[:].rearrange("p c n -> p n c")
 
-        a_right = keep.tile([P, M], F32, name="a_right", tag="a_right_then_words", align_bytes=64)
-        dl = keep.tile([P, M], F32, name="dl")
-        nc.vector.tensor_copy(a_right[:], a_sb[:].indirect(right_list[:]))
-        nc.vector.tensor_tensor(dl[:], a_sb[:].indirect(left_list[:]), a_right[:], ALU.subtract)
-        sq = keep.tile([P, M], F32, name="sq")
-        nc.scalar.activation(sq[:], dl[:], ACT.Square)
+        def pairs(t):
+            return t[:].rearrange("p (n c) -> p n c", c=2)
 
-        dtab_w = keep.tile([P, J], U32, name="dtab_w", tag="a_right_then_words", align_bytes=64)
-        nc.vector.tensor_copy(dtab_w[:], dtab_sb[:].bitcast(U32).indirect(slot_list[:]))
         ta_ps = psum.tile([P, J], F32, name="ta_ps")
         nc.tensor.matmul_mx(ta_ps[:], lhsT=w_codes[:].bitcast(FP8X4), lhsT_scale=w_scales[:], rhs=dtab_w[:].bitcast(FP8X4), rhs_scale=dtab_s[4:P, :], start=True, stop=True)
         ta_sb = keep.tile([P, J], F32, name="ta_sb")
         nc.scalar.copy(ta_sb[:], ta_ps[:])
 
-        def pairs(t):
-            return t[:].rearrange("p (n c) -> p n c", c=2)
+        a_right = reuse.tile([P, M], F32, name="a_right", offset=T - 2 * M)
+        dl = keep.tile([P, M], F32, name="dl")
+        nc.vector.tensor_copy(a_right[:], a_sb[:].indirect(right_list[:]))
+        nc.vector.tensor_tensor(dl[:], a_sb[:].indirect(left_list[:]), a_right[:], ALU.subtract)
+        sq = keep.tile([P, M], F32, name="sq", tag="sq_then_tdl")
+        nc.scalar.activation(sq[:], dl[:], ACT.Square)
+        ta_right = keep.tile([P, M], F32, name="ta_right")
+        nc.vector.tensor_copy(ta_right[:], ta_sb[:].indirect(right_list[:]))
 
-        e = reuse.tile([P, M], F32, name="e", offset=0)
+        e = keep.tile([P, M], F32, name="e")
         nc.vector.tensor_tensor(pairs(e), pairs(sq), sharp_row, ALU.mult)
         u = keep.tile([P, M], F32, name="u")
         nc.scalar.activation(u[:], e[:], ACT.Exp, scale=-1.0)
-        q = reuse.tile([P, M], F32, name="q", offset=4 * M)
+        q = keep.tile([P, M], F32, name="q")
         nc.vector.scalar_tensor_tensor(pairs(q), pairs(dl), -2.0, sharp_row, ALU.mult, ALU.mult)
+        tdl = keep.tile([P, M], F32, name="tdl", tag="sq_then_tdl")
+        nc.vector.tensor_tensor(tdl[:], ta_sb[:].indirect(left_list[:]), ta_right[:], ALU.subtract)
         c = keep.tile([P, M], F32, name="c")
         nc.vector.tensor_tensor(c[:], q[:], u[:], ALU.mult)
-
-        ta_right = keep.tile([P, M], F32, name="ta_right")
-        nc.vector.tensor_copy(ta_right[:], ta_sb[:].indirect(right_list[:]))
-        tdl = keep.tile([P, M], F32, name="tdl")
-        nc.vector.tensor_tensor(tdl[:], ta_sb[:].indirect(left_list[:]), ta_right[:], ALU.subtract)
         m = keep.tile([P, M], F32, name="m")
         nc.vector.tensor_tensor(m[:], c[:], tdl[:], ALU.mult)
         y = keep.tile([P, M], F32, name="y")

@@ -31,14 +31,16 @@ def tile_attend_tcpairnear_kernel(tc, tab_words, tab_scales, dtab_words, dtab_sc
         left_list = lists.tile([P, M // 16], U16, name="left_list")
         right_list = lists.tile([P, M // 16], U16, name="right_list")
         nc.sync.dma_start(slot_list[:], offs)
-        w_raw = reuse.tile([P, PACK, R], F32, name="w_raw", offset=T)
+        w_raw = keep.tile([P, PACK, R], F32, name="w_raw")
         nc.scalar.dma_start(w_raw[:], w1.rearrange("(p j) r -> p j r", j=PACK))
         nc.sync.dma_start(left_list[:], offs2)
+        sharp_col = keep.tile([P, 2], F32, name="sharp_col")
+        nc.scalar.dma_start(sharp_col[:], sharp.rearrange("o (p c) -> (o p) c", c=2))
+        nc.sync.dma_start(right_list[:], offs3)
         tab_sb = keep.tile([P, T], I32, name="tab_sb")
         nc.scalar.dma_start(tab_sb[:], tab_words[0].rearrange("p n t -> p (n t)").bitcast(I32))
-        nc.sync.dma_start(right_list[:], offs3)
 
-        late_at = 5 * T
+        late_at = 6 * T
         tab_plane = reuse.tile([P, T], U8, name="tab_plane", offset=late_at)
         dtab_plane = reuse.tile([P, T], U8, name="dtab_plane", offset=0)
         nc.vector.memset(tab_plane[:].bitcast(I32), 0)
@@ -55,39 +57,37 @@ def tile_attend_tcpairnear_kernel(tc, tab_words, tab_scales, dtab_words, dtab_sc
         ident = keep.tile([P, P], F32, name="ident")
         make_identity(nc, ident[:])
 
-        w_bf = keep.tile([P, R, PACK], BF16, name="w_bf", align_bytes=64)
+        sharp_ps = psum.tile([P, 2, P], F32, name="sharp_ps")
+        for half in range(2):
+            nc.tensor.transpose(sharp_ps[:, half, :], sharp_col[:, half : half + 1].to_broadcast([P, P]), ident[:])
+        sharp_row = sharp_ps[:].rearrange("p c n -> p n c")
+
+        w_bf = reuse.tile([P, R, PACK], BF16, name="w_bf", offset=5 * T - 512, align_bytes=64)
         nc.scalar.copy(w_bf[:], w_raw[:].rearrange("p j r -> p r j"))
-        dtab_sb = reuse.tile([P, T], I32, name="dtab_sb", offset=T)
-        nc.scalar.dma_start(dtab_sb[:], dtab_words[0].rearrange("p n t -> p (n t)").bitcast(I32))
         w_codes = keep.tile([P, R], U32, name="w_codes", align_bytes=64)
         w_scales = keep.tile([P, R], U8, name="w_scales", align_bytes=64)
         nc.vector.quantize_mx(w_codes[:].bitcast(FP8X4), w_scales[:], w_bf[:].rearrange("p r j -> p (r j)"))
 
+        dtab_sb = reuse.tile([P, T], I32, name="dtab_sb", offset=T)
+        nc.scalar.dma_start(dtab_sb[:], dtab_words[0].rearrange("p n t -> p (n t)").bitcast(I32))
         tab_s = keep.tile([P, J], U8, name="tab_s", align_bytes=64)
         nc.vector.tensor_copy(tab_s[:], tab_plane[:].indirect(slot_list[:]))
-        sharp_col = reuse.tile([P, 2], F32, name="sharp_col", offset=late_at)
-        nc.sync.dma_start(sharp_col[:], sharp.rearrange("o (p c) -> (o p) c", c=2))
         og_col = reuse.tile([P, 1], F32, name="og_col", offset=late_at + 32)
         nc.sync.dma_start(og_col[:], og)
         base_sb = reuse.tile([P, M], F32, name="base_sb", offset=late_at + 64)
         nc.sync.dma_start(base_sb[:], base)
 
-        tab_w = keep.tile([P, J], U32, name="tab_w", align_bytes=64)
+        tab_w = reuse.tile([P, J], U32, name="tab_w", offset=5 * T, align_bytes=64)
         nc.vector.tensor_copy(tab_w[:], tab_sb[:].bitcast(U32).indirect(slot_list[:]))
         dtab_s = keep.tile([P, J], U8, name="dtab_s", align_bytes=64)
         nc.vector.tensor_copy(dtab_s[:], dtab_plane[:].indirect(slot_list[:]))
         dtab_w = keep.tile([P, J], U32, name="dtab_w", align_bytes=64)
         nc.vector.tensor_copy(dtab_w[:], dtab_sb[:].bitcast(U32).indirect(slot_list[:]))
 
-        a_ps = psum.tile([P, J], F32, name="a_ps", tag="a_then_sharp")
+        a_ps = psum.tile([P, J], F32, name="a_ps")
         nc.tensor.matmul_mx(a_ps[:], lhsT=w_codes[:].bitcast(FP8X4), lhsT_scale=w_scales[:], rhs=tab_w[:].bitcast(FP8X4), rhs_scale=tab_s[:], start=True, stop=True)
         a_sb = keep.tile([P, J], F32, name="a_sb")
         nc.scalar.copy(a_sb[:], a_ps[:])
-
-        sharp_ps = psum.tile([P, 2, P], F32, name="sharp_ps", tag="a_then_sharp")
-        for half in range(2):
-            nc.tensor.transpose(sharp_ps[:, half, :], sharp_col[:, half : half + 1].to_broadcast([P, P]), ident[:])
-        sharp_row = sharp_ps[:].rearrange("p c n -> p n c")
 
         def pairs(t):
             return t[:].rearrange("p (n c) -> p n c", c=2)

@@ -34,14 +34,12 @@ def tile_attend_tcpairnear_kernel(tc, tab_words, tab_scales, dtab_words, dtab_sc
         w_raw = keep.tile([P, PACK, R], F32, name="w_raw")
         nc.scalar.dma_start(w_raw[:], w1.rearrange("(p j) r -> p j r", j=PACK))
         nc.sync.dma_start(left_list[:], offs2)
-        sharp_col = keep.tile([P, 2], F32, name="sharp_col")
-        nc.scalar.dma_start(sharp_col[:], sharp.rearrange("o (p c) -> (o p) c", c=2))
-        nc.sync.dma_start(right_list[:], offs3)
         tab_sb = keep.tile([P, T], I32, name="tab_sb")
         nc.scalar.dma_start(tab_sb[:], tab_words[0].rearrange("p n t -> p (n t)").bitcast(I32))
+        nc.sync.dma_start(right_list[:], offs3)
 
         late_at = 6 * T
-        tab_plane = reuse.tile([P, T], U8, name="tab_plane", offset=late_at)
+        tab_plane = reuse.tile([P, T], U8, name="tab_plane", offset=late_at - 64)
         dtab_plane = reuse.tile([P, T], U8, name="dtab_plane", offset=0)
         nc.vector.memset(tab_plane[:].bitcast(I32), 0)
         nc.vector.memset(dtab_plane[:].bitcast(I32), 0)
@@ -57,11 +55,6 @@ def tile_attend_tcpairnear_kernel(tc, tab_words, tab_scales, dtab_words, dtab_sc
         ident = keep.tile([P, P], F32, name="ident")
         make_identity(nc, ident[:])
 
-        sharp_ps = psum.tile([P, 2, P], F32, name="sharp_ps")
-        for half in range(2):
-            nc.tensor.transpose(sharp_ps[:, half, :], sharp_col[:, half : half + 1].to_broadcast([P, P]), ident[:])
-        sharp_row = sharp_ps[:].rearrange("p c n -> p n c")
-
         w_bf = reuse.tile([P, R, PACK], BF16, name="w_bf", offset=5 * T - 512, align_bytes=64)
         nc.scalar.copy(w_bf[:], w_raw[:].rearrange("p j r -> p r j"))
         w_codes = keep.tile([P, R], U32, name="w_codes", align_bytes=64)
@@ -72,6 +65,8 @@ def tile_attend_tcpairnear_kernel(tc, tab_words, tab_scales, dtab_words, dtab_sc
         nc.scalar.dma_start(dtab_sb[:], dtab_words[0].rearrange("p n t -> p (n t)").bitcast(I32))
         tab_s = keep.tile([P, J], U8, name="tab_s", align_bytes=64)
         nc.vector.tensor_copy(tab_s[:], tab_plane[:].indirect(slot_list[:]))
+        sharp_col = reuse.tile([P, 2], F32, name="sharp_col", offset=late_at)
+        nc.sync.dma_start(sharp_col[:], sharp.rearrange("o (p c) -> (o p) c", c=2))
         og_col = reuse.tile([P, 1], F32, name="og_col", offset=late_at + 32)
         nc.sync.dma_start(og_col[:], og)
         base_sb = reuse.tile([P, M], F32, name="base_sb", offset=late_at + 64)
@@ -84,10 +79,15 @@ def tile_attend_tcpairnear_kernel(tc, tab_words, tab_scales, dtab_words, dtab_sc
         dtab_w = keep.tile([P, J], U32, name="dtab_w", align_bytes=64)
         nc.vector.tensor_copy(dtab_w[:], dtab_sb[:].bitcast(U32).indirect(slot_list[:]))
 
-        a_ps = psum.tile([P, J], F32, name="a_ps")
+        a_ps = psum.tile([P, J], F32, name="a_ps", tag="a_then_sharp")
         nc.tensor.matmul_mx(a_ps[:], lhsT=w_codes[:].bitcast(FP8X4), lhsT_scale=w_scales[:], rhs=tab_w[:].bitcast(FP8X4), rhs_scale=tab_s[:], start=True, stop=True)
         a_sb = keep.tile([P, J], F32, name="a_sb")
         nc.scalar.copy(a_sb[:], a_ps[:])
+
+        sharp_ps = psum.tile([P, 2, P], F32, name="sharp_ps", tag="a_then_sharp")
+        for half in range(2):
+            nc.tensor.transpose(sharp_ps[:, half, :], sharp_col[:, half : half + 1].to_broadcast([P, P]), ident[:])
+        sharp_row = sharp_ps[:].rearrange("p c n -> p n c")
 
         def pairs(t):
             return t[:].rearrange("p (n c) -> p n c", c=2)

from contextlib import ExitStack

import concourse.mybir as mybir
from concourse.masks import make_identity

K, R, T, J, M = 512, 128, 2048, 512, 256
FLOPS = 2 * 2 * K * R * J

F32 = mybir.dt.float32
BF16 = mybir.dt.bfloat16
I32 = mybir.dt.int32
U32 = mybir.dt.uint32
U16 = mybir.dt.uint16
U8 = mybir.dt.uint8
FP8X4 = mybir.dt.float8_e4m3fn_x4
ALU = mybir.AluOpType
ACT = mybir.ActivationFunctionType
P = 128
PACK = 4


def tile_attend_tcpairnear_kernel(tc, tab_words, tab_scales, dtab_words, dtab_scales, w1, sharp, og, base, offs, offs2, offs3, out):
    nc = tc.nc
    with ExitStack() as ctx:
        lists = ctx.enter_context(tc.tile_pool(name="lists", bufs=1))
        keep = ctx.enter_context(tc.tile_pool(name="keep", bufs=1))
        reuse = ctx.enter_context(tc.tile_pool(name="reuse", bufs=1))
        psum = ctx.enter_context(tc.psum_pool(name="psum", bufs=1))

        slot_list = lists.tile([P, J // 16], U16, name="slot_list")
        left_list = lists.tile([P, M // 16], U16, name="left_list")
        right_list = lists.tile([P, M // 16], U16, name="right_list")
        nc.sync.dma_start(slot_list[:], offs)
        w_raw = keep.tile([P, PACK, R], F32, name="w_raw")
        nc.scalar.dma_start(w_raw[:], w1.rearrange("(p j) r -> p j r", j=PACK))
        nc.sync.dma_start(left_list[:], offs2)
        tab_sb = keep.tile([P, T], I32, name="tab_sb")
        nc.scalar.dma_start(tab_sb[:], tab_words[0].rearrange("p n t -> p (n t)").bitcast(I32))
        nc.sync.dma_start(right_list[:], offs3)

        late_at = 6 * T
        tab_plane = reuse.tile([P, T], U8, name="tab_plane", offset=late_at - 64)
        dtab_plane = reuse.tile([P, T], U8, name="dtab_plane", offset=0)
        nc.vector.memset(tab_plane[:].bitcast(I32), 0)
        nc.vector.memset(dtab_plane[:].bitcast(I32), 0)

        def load_plane(plane, scales, first_row):
            rows = scales[0].bitcast(I32).rearrange("(q f) c -> f q c", f=4)
            for f in range(4):
                nc.sync.dma_start(plane[:].bitcast(I32)[first_row + f : P : 32, :], rows[f])

        load_plane(tab_plane, tab_scales, 0)
        load_plane(dtab_plane, dtab_scales, 4)

        ident = keep.tile([P, P], F32, name="ident")
        make_identity(nc, ident[:])

        w_bf = reuse.tile([P, R, PACK], BF16, name="w_bf", offset=5 * T - 512, align_bytes=64)
        nc.scalar.copy(w_bf[:], w_raw[:].rearrange("p j r -> p r j"))
        w_codes = keep.tile([P, R], U32, name="w_codes", align_bytes=64)
        w_scales = keep.tile([P, R], U8, name="w_scales", align_bytes=64)
        nc.vector.quantize_mx(w_codes[:].bitcast(FP8X4), w_scales[:], w_bf[:].rearrange("p r j -> p (r j)"))

        dtab_sb = reuse.tile([P, T], I32, name="dtab_sb", offset=T)
        nc.scalar.dma_start(dtab_sb[:], dtab_words[0].rearrange("p n t -> p (n t)").bitcast(I32))
        tab_s = keep.tile([P, J], U8, name="tab_s", align_bytes=64)
        nc.vector.tensor_copy(tab_s[:], tab_plane[:].indirect(slot_list[:]))
        sharp_col = reuse.tile([P, 2], F32, name="sharp_col", offset=late_at)
        nc.sync.dma_start(sharp_col[:], sharp.rearrange("o (p c) -> (o p) c", c=2))
        og_col = reuse.tile([P, 1], F32, name="og_col", offset=late_at + 32)
        nc.sync.dma_start(og_col[:], og)
        base_sb = reuse.tile([P, M], F32, name="base_sb", offset=late_at + 64)
        nc.sync.dma_start(base_sb[:], base)

        tab_w = reuse.tile([P, J], U32, name="tab_w", offset=5 * T, align_bytes=64)
        nc.vector.tensor_copy(tab_w[:], tab_sb[:].bitcast(U32).indirect(slot_list[:]))
        dtab_s = keep.tile([P, J], U8, name="dtab_s", align_bytes=64)
        nc.vector.tensor_copy(dtab_s[:], dtab_plane[:].indirect(slot_list[:]))
        dtab_w = keep.tile([P, J], U32, name="dtab_w", align_bytes=64)
        nc.vector.tensor_copy(dtab_w[:], dtab_sb[:].bitcast(U32).indirect(slot_list[:]))

        a_ps = psum.tile([P, J], F32, name="a_ps", tag="a_then_sharp")
        nc.tensor.matmul_mx(a_ps[:], lhsT=w_codes[:].bitcast(FP8X4), lhsT_scale=w_scales[:], rhs=tab_w[:].bitcast(FP8X4), rhs_scale=tab_s[:], start=True, stop=True)
        a_sb = keep.tile([P, J], F32, name="a_sb")
        nc.scalar.copy(a_sb[:], a_ps[:])

        sharp_ps = psum.tile([P, 2, P], F32, name="sharp_ps", tag="a_then_sharp")
        for half in range(2):
            nc.tensor.transpose(sharp_ps[:, half, :], sharp_col[:, half : half + 1].to_broadcast([P, P]), ident[:])
        sharp_row = sharp_ps[:].rearrange("p c n -> p n c")

        def pairs(t):
            return t[:].rearrange("p (n c) -> p n c", c=2)

        ta_ps = psum.tile([P, J], F32, name="ta_ps")
        nc.tensor.matmul_mx(ta_ps[:], lhsT=w_codes[:].bitcast(FP8X4), lhsT_scale=w_scales[:], rhs=dtab_w[:].bitcast(FP8X4), rhs_scale=dtab_s[4:P, :], start=True, stop=True)
        ta_sb = keep.tile([P, J], F32, name="ta_sb")
        nc.scalar.copy(ta_sb[:], ta_ps[:])

        a_right = reuse.tile([P, M], F32, name="a_right", offset=T - 2 * M)
        dl = keep.tile([P, M], F32, name="dl")
        nc.vector.tensor_copy(a_right[:], a_sb[:].indirect(right_list[:]))
        nc.vector.tensor_tensor(dl[:], a_sb[:].indirect(left_list[:]), a_right[:], ALU.subtract)
        sq = keep.tile([P, M], F32, name="sq", tag="sq_then_tdl")
        nc.scalar.activation(sq[:], dl[:], ACT.Square)
        ta_right = keep.tile([P, M], F32, name="ta_right")
        nc.vector.tensor_copy(ta_right[:], ta_sb[:].indirect(right_list[:]))

        e = keep.tile([P, M], F32, name="e")
        nc.vector.tensor_tensor(pairs(e), pairs(sq), sharp_row, ALU.mult)
        u = keep.tile([P, M], F32, name="u")
        nc.scalar.activation(u[:], e[:], ACT.Exp, scale=-1.0)
        q = keep.tile([P, M], F32, name="q")
        nc.vector.scalar_tensor_tensor(pairs(q), pairs(dl), -2.0, sharp_row, ALU.mult, ALU.mult)
        tdl = keep.tile([P, M], F32, name="tdl", tag="sq_then_tdl")
        nc.vector.tensor_tensor(tdl[:], ta_sb[:].indirect(left_list[:]), ta_right[:], ALU.subtract)
        c = keep.tile([P, M], F32, name="c")
        nc.vector.tensor_tensor(c[:], q[:], u[:], ALU.mult)
        m = keep.tile([P, M], F32, name="m")
        nc.vector.tensor_tensor(m[:], c[:], tdl[:], ALU.mult)
        y = keep.tile([P, M], F32, name="y")
        nc.vector.scalar_tensor_tensor(y[:], m[:], og_col[:], base_sb[:], ALU.mult, ALU.add)
        nc.sync.dma_start(out, y[:])
